import numpy as np
import ml_dtypes


def mxq(x, axis, fmt="e4m3"):
    dtype, down = {"e4m3": (ml_dtypes.float8_e4m3fn, 7), "e5m2": (ml_dtypes.float8_e5m2, 14)}[fmt]
    v = np.moveaxis(np.asarray(x, np.float32).astype(ml_dtypes.bfloat16).astype(np.float64), axis, -1)
    blocks = v.reshape(v.shape[:-1] + (-1, 32))
    amax = np.abs(blocks).max(-1, keepdims=True)
    byte = np.maximum(np.where(amax > 0, np.frexp(amax)[1] - 1 + 127, 0) - down, 1)
    scale = np.exp2(byte - 127.0)
    codes = (blocks / scale).astype(np.float32).astype(dtype).astype(np.float64)
    return np.moveaxis((codes * scale).reshape(v.shape), -1, axis)


WIDE = False


def mx_kscale(k):
    if not WIDE:
        return np.ones(k)
    levels = np.array([10, -10, 5, -5, 0])
    if k % 512:
        return np.exp2(np.random.permutation(np.resize(levels, k // 32))).repeat(32)
    a = np.empty((k // 512, 16))
    for p in range(k // 512):
        a[p, :8] = np.random.permutation(np.resize(levels, 8))
        for g in range(8):
            far = levels[np.abs(levels - a[p, g]) >= 10]
            a[p, g + 8] = far[np.random.randint(len(far))]
    return np.exp2(a.ravel()).repeat(32)


def f64(x):
    return np.asarray(x).astype(np.float64)


def striped(idx):
    return np.tile(idx.reshape(-1, 16).T, (8, 1)).astype(np.uint16)


def unstriped(offs):
    return offs[:16].T.reshape(-1).astype(np.int64)


E2M1 = np.array([0.0, 0.5, 1.0, 1.5, 2.0, 3.0, 4.0, 6.0, -0.0, -0.5, -1.0, -1.5, -2.0, -3.0, -4.0, -6.0])


def pack_weight(w, fmt):
    k, n = w.shape
    w = f64(np.asarray(w, np.float32).astype(ml_dtypes.bfloat16)).reshape(k // 32, 32, n)
    amax = np.abs(w).max(1)
    if fmt == "e4m3":
        byte = np.frexp(amax)[1] - 1 + 127 - 7
    else:
        mant, ex = np.frexp(amax / 6.0)
        byte = np.where(mant > 0.5, ex, ex - 1) + 127
    byte = np.clip(np.where(amax > 0, byte, 1), 1, 254)
    scaled = (w * np.exp2(127.0 - byte)[:, None, :]).reshape(k, n).astype(np.float32)
    by_word = np.ascontiguousarray(scaled.reshape(k // 512, 128, 4, n).transpose(0, 1, 3, 2))
    if fmt == "e4m3":
        words = by_word.astype(ml_dtypes.float8_e4m3fn).view(np.uint8)
    else:
        c = by_word.astype(ml_dtypes.float4_e2m1fn).view(np.uint8) & 0xF
        words = (c[..., 0::2] | (c[..., 1::2] << 4)).reshape(k // 512, 128, 2 * n)
    return np.ascontiguousarray(words), np.ascontiguousarray(byte.astype(np.uint8).reshape(k // 512, 16, n))


def unpack_weight(words, scales, fmt):
    g, _, n = scales.shape
    words = np.ascontiguousarray(words).reshape(g, 128, n, -1)
    if fmt == "e4m3":
        vals = words.view(ml_dtypes.float8_e4m3fn).astype(np.float64)
    else:
        nib = np.empty((g, 128, n, 4), np.uint8)
        nib[..., 0::2] = words & 0xF
        nib[..., 1::2] = words >> 4
        vals = E2M1[nib]
    vals = vals * np.repeat(np.exp2(scales.astype(np.float64) - 127.0), 8, axis=1)[..., None]
    return vals.transpose(0, 1, 3, 2).reshape(g * 512, n)


def gelu(v):
    return 0.5 * v * (1.0 + np.tanh(np.sqrt(2.0 / np.pi) * (v + 0.044715 * v**3)))


def striped8(idx):
    return np.concatenate([v.reshape(-1, 16).T for v in idx]).astype(np.uint16)


def unstriped8(offs):
    return np.stack([offs[16 * g:16 * g + 16].T.reshape(-1) for g in range(8)]).astype(np.int64)


def runs(v, idx8):
    k = np.arange(v.shape[0])
    return v[k[:, None], idx8[k % 512 // 64]]


K, T, S, H, P, N = 1536, 4096, 1024, 512, 512, 768


def setup_inputs():
    n = np.random.standard_normal
    s = mx_kscale(K)[:, None]
    u = mx_kscale(H)[:, None]
    tab_words, tab_scales = pack_weight(n((K, T)) * s, "e4m3")
    w2_words, w2_scales = pack_weight(1.3 * n((K, H)) / np.sqrt(K) / s, "e2m1")
    arms = np.stack([np.random.permutation(S)[:P] for _ in range(8)])
    return {
        "tab_words": tab_words, "tab_scales": tab_scales,
        "offs": striped(np.random.permutation(T)[:S]),
        "offs2": striped8(arms),
        "w1": (0.65 * n((K, H)) / np.sqrt(K) / s).astype(np.float32),
        "w2_words": w2_words, "w2_scales": w2_scales,
        "b2": (0.5 * n(H)).astype(np.float32),
        "sc": np.repeat(np.random.uniform(0.6, 3.0, H // 64), 64).astype(np.float32),
        "th": np.repeat(n(H // 64), 64).astype(np.float32),
        "gain": (np.random.uniform(0.8, 2.4, H) * u[:, 0]).astype(np.float32),
        "w3": (n((H, N)) / np.sqrt(H) / u).astype(np.float32),
        "low": (0.8 * n((N, P))).astype(np.float32),
    }


def reference(tab_words, tab_scales, offs, offs2, w1, w2_words, w2_scales, b2, sc, th, gain, w3, low):
    v = unpack_weight(tab_words, tab_scales, "e4m3")[:, unstriped(offs)]
    y1 = mxq(f64(w1), 0, "e4m3").T @ v
    y2 = unpack_weight(w2_words, w2_scales, "e2m1").T @ v
    h = y1 + np.tanh(y2 + f64(b2)[:, None])
    hp = runs(h, unstriped8(offs2))
    a = 1.0 / (1.0 + np.exp(-(f64(sc)[:, None] * hp + f64(th)[:, None])))
    e = f64(gain)[:, None] * np.minimum(a, hp)
    y3 = mxq(f64(w3), 0, "e4m3").T @ mxq(e, 0, "e4m3")
    return np.maximum(y3, f64(low))

@@ -1,0 +1,251 @@
+from contextlib import ExitStack
+
+import concourse.mybir as mybir
+
+K, T, S, H, M, N = 1536, 4096, 1024, 512, 512, 768
+FLOPS = 2 * K * H * S * 2 + 2 * H * N * M
+
+F32 = mybir.dt.float32
+BF16 = mybir.dt.bfloat16
+I32 = mybir.dt.int32
+U32 = mybir.dt.uint32
+U16 = mybir.dt.uint16
+U8 = mybir.dt.uint8
+FP8X4 = mybir.dt.float8_e4m3fn_x4
+FP4X4 = mybir.dt.float4_e2m1fn_x4
+ACT = mybir.ActivationFunctionType
+ALU = mybir.AluOpType
+
+P = 128
+PACK = 4
+PASSES = K // (P * PACK)
+BANK = 512
+S_HALVES = S // BANK
+M_HALF = M // 2
+N_HALF = N // 2
+SHIFT_ROWS = 112
+
+
+def tile_list_arm_leak_scores_kernel(
+    tc, tab_words, tab_scales, offs, offs2, w1, w2_words, w2_scales, b2, sc, th, gain, w3, low, out
+):
+    nc = tc.nc
+    with ExitStack() as ctx:
+        sb = ctx.enter_context(tc.tile_pool(name="sb", bufs=1))
+        psum = ctx.enter_context(tc.psum_pool(name="psum", bufs=1))
+
+        def sbt(name, shape, dtype):
+            return sb.tile(shape, dtype, name=name, align_bytes=64)
+
+        idx = sbt("idx", [P, S // 16], U16)
+        nc.sync.dma_start(idx[:], offs)
+        w2_raw = sbt("w2_raw", [P, PASSES, 2 * H], U8)
+        nc.sync.dma_start(w2_raw[:].bitcast(I32), w2_words.rearrange("a p c -> p a c").bitcast(I32))
+        tab = []
+        for a in range(PASSES):
+            tab.append(sbt(f"tab{a}", [P, T], U32))
+            nc.sync.dma_start(tab[a][:].bitcast(I32), tab_words[a].rearrange("p t i -> p (t i)").bitcast(I32))
+
+        def load_rows(name, vec):
+            t = sbt(name, [P, PACK], F32)
+            nc.scalar.dma_start(t[:], vec.rearrange("(p i) -> p i", i=PACK))
+            return t
+
+        idx2 = sbt("idx2", [P, M // 16], U16)
+        nc.sync.dma_start(idx2[:], offs2)
+        b2_sb = load_rows("b2_sb", b2)
+        w1_rows = w1.rearrange("(a p j) c -> a p j c", p=P, j=PACK)
+        w1_raw = []
+        for a in range(PASSES - 1):
+            w1_raw.append(sbt(f"w1_raw{a}", [P, PACK, H], F32))
+            nc.sync.dma_start(w1_raw[a][:], w1_rows[a])
+        w1_last = []
+        for u in range(2):
+            w1_last.append(sbt(f"w1_last{u}", [P, PACK, H // 2], F32))
+            nc.sync.dma_start(w1_last[u][:], w1_rows[PASSES - 1][:, :, u * (H // 2) : (u + 1) * (H // 2)])
+        sc_sb = load_rows("sc_sb", sc)
+        th_sb = load_rows("th_sb", th)
+        gain_sb = load_rows("gain_sb", gain)
+        w3_rows = w3.rearrange("(p j) n -> p j n", j=PACK)
+        w3_raw = []
+        for u in range(2):
+            w3_raw.append(sbt(f"w3_raw{u}", [P, PACK, N_HALF], F32))
+            nc.sync.dma_start(w3_raw[u][:], w3_rows[:, :, u * N_HALF : (u + 1) * N_HALF])
+        low_rows = low.rearrange("(g t p) m -> g p t m", t=2, p=P)
+        out_rows = out.rearrange("(g t p) m -> g p t m", t=2, p=P)
+        score = []
+        for g in range(N // (2 * P)):
+            score.append(sbt(f"score{g}", [P, 2, M], F32))
+            nc.sync.dma_start(score[g][:], low_rows[g])
+
+        tab_sc = sbt("tab_sc", [P, T], U8)
+        nc.gpsimd.memset(tab_sc[:].bitcast(I32), 0)
+        for q in range(4):
+            nc.gpsimd.dma_start(
+                tab_sc[32 * q : 32 * q + 4 * PASSES, :].bitcast(I32), tab_scales[:, 4 * q : 4 * q + 4, :].bitcast(I32)
+            )
+        w2_sc_raw = sbt("w2_sc_raw", [P, PASSES, H], U8)
+        nc.gpsimd.memset(w2_sc_raw[:].bitcast(I32), 0)
+        for q in range(4):
+            nc.gpsimd.dma_start(
+                w2_sc_raw[32 * q : 32 * q + 4, :, :].bitcast(I32),
+                w2_scales[:, 4 * q : 4 * q + 4, :].rearrange("a r c -> r a c").bitcast(I32),
+            )
+        v_sc_low = {}
+        for a in range(1, PASSES):
+            v_sc_low[a] = sbt(f"v_sc_low{a}", [P, S], U8)
+            nc.gpsimd.memset(v_sc_low[a][:].bitcast(I32), 0)
+
+        w2_codes = sbt("w2_codes", [P, PASSES, 2 * H], U8)
+        nc.vector.tensor_copy(
+            w2_codes[:].rearrange("p a (i m b) -> p a m i b", i=PACK, b=2),
+            w2_raw[:].rearrange("p a (m i b) -> p a m i b", i=PACK, b=2),
+        )
+        w2_sc = sbt("w2_sc", [P, PASSES, H], U8)
+        nc.vector.tensor_copy(
+            w2_sc[:].rearrange("p a (i m) -> p a m i", i=PACK),
+            w2_sc_raw[:].rearrange("p a (m i) -> p a m i", i=PACK),
+        )
+
+        v_sc = sbt("v_sc", [P, S], U8)
+        nc.vector.tensor_copy(v_sc[:], tab_sc[:].indirect(idx[:]))
+        for a in range(1, PASSES):
+            nc.gpsimd.dma_start(
+                v_sc_low[a][0:SHIFT_ROWS, :].bitcast(I32), v_sc[4 * a : 4 * a + SHIFT_ROWS, :].bitcast(I32)
+            )
+        v_sc_low[0] = v_sc
+
+        y2 = {}
+        v_codes = {}
+        for a in range(PASSES):
+            for s in range(S_HALVES):
+                v_codes[a, s] = sbt(f"v_codes{a}_{s}", [P, BANK], U32)
+                nc.vector.tensor_copy(
+                    v_codes[a, s][:], tab[a][:].indirect(idx[:, s * (BANK // 16) : (s + 1) * (BANK // 16)])
+                )
+                for i in range(PACK):
+                    if a == 0:
+                        y2[i, s] = psum.tile([P, BANK], F32, name=f"bank{S_HALVES * i + s}")
+                    nc.tensor.matmul_mx(
+                        out=y2[i, s][:],
+                        lhsT=w2_codes[:, a, 2 * P * i : 2 * P * (i + 1)].bitcast(FP4X4),
+                        lhsT_scale=w2_sc[:, a, P * i : P * (i + 1)],
+                        rhs=v_codes[a, s][:].bitcast(FP8X4),
+                        rhs_scale=v_sc_low[a][:, s * BANK : (s + 1) * BANK],
+                        start=(a == 0),
+                        stop=(a == PASSES - 1),
+                    )
+
+        h = [sbt(f"h{i}", [P, S], F32) for i in range(PACK)]
+        bent = sbt("stage", [P, PACK, S], F32)
+        for s in range(S_HALVES):
+            for i in range(PACK):
+                nc.scalar.activation(
+                    out=bent[:, i, s * BANK : (s + 1) * BANK], in_=y2[i, s][:], func=ACT.Tanh, bias=b2_sb[:, i : i + 1]
+                )
+
+        w1_bf = [sbt(f"w1_bf{a}", [P, PACK, P, PACK], BF16) for a in range(PASSES)]
+        w1_codes = [sbt(f"w1_codes{a}", [P, H], U32) for a in range(PASSES)]
+        w1_sc = [sbt(f"w1_sc{a}", [P, H], U8) for a in range(PASSES)]
+        for a in range(PASSES - 1):
+            nc.vector.tensor_copy(
+                w1_bf[a][:].rearrange("p i m j -> p m j i"), w1_raw[a][:].rearrange("p j (m i) -> p m j i", i=PACK)
+            )
+            nc.vector.quantize_mx(
+                out=w1_codes[a][:].bitcast(FP8X4), scales=w1_sc[a][:], in_=w1_bf[a][:].rearrange("p i m j -> p (i m j)")
+            )
+        last = PASSES - 1
+        nc.scalar.copy(
+            w1_bf[last][:, :, 0 : P // 2, :].rearrange("p i m j -> p m j i"),
+            w1_last[0][:].rearrange("p j (m i) -> p m j i", i=PACK),
+        )
+        nc.vector.tensor_copy(
+            w1_bf[last][:, :, P // 2 : P, :].rearrange("p i m j -> p m j i"),
+            w1_last[1][:].rearrange("p j (m i) -> p m j i", i=PACK),
+        )
+
+        y1 = {}
+
+        def y1_pass(i, s, a):
+            nc.tensor.matmul_mx(
+                out=y1[i, s][:],
+                lhsT=w1_codes[a][:, P * i : P * (i + 1)].bitcast(FP8X4),
+                lhsT_scale=w1_sc[a][:, P * i : P * (i + 1)],
+                rhs=v_codes[a, s][:].bitcast(FP8X4),
+                rhs_scale=v_sc[4 * a : P, s * BANK : (s + 1) * BANK],
+                start=(a == 0),
+                stop=(a == last),
+            )
+
+        for s in range(S_HALVES):
+            for i in range(PACK):
+                y1[i, s] = psum.tile([P, BANK], F32, name=f"bank{S_HALVES * i + s}")
+                y1_pass(i, s, 0)
+        for i in range(PACK):
+            nc.vector.quantize_mx(
+                out=w1_codes[last][:, P * i : P * (i + 1)].bitcast(FP8X4),
+                scales=w1_sc[last][:, P * i : P * (i + 1)],
+                in_=w1_bf[last][:, i, :, :].rearrange("p m j -> p (m j)"),
+            )
+        for i in range(PACK):
+            for a in range(1, PASSES):
+                for s in range(S_HALVES):
+                    y1_pass(i, s, a)
+            for s in range(S_HALVES):
+                cols = slice(s * BANK, (s + 1) * BANK)
+                nc.vector.tensor_tensor(h[i][:, cols], y1[i, s][:], bent[:, i, cols], ALU.add)
+
+        w3_codes = []
+        w3_sc = []
+        for u in range(2):
+            w3_bf = sbt(f"w3_bf{u}", [P, N_HALF, PACK], BF16)
+            nc.gpsimd.tensor_scalar(
+                w3_bf[:], w3_raw[u][:].rearrange("p j n -> p n j"), 1.0, 0.0, ALU.mult, ALU.add
+            )
+            w3_codes.append(sbt(f"w3_codes{u}", [P, N_HALF], U32))
+            w3_sc.append(sbt(f"w3_sc{u}", [P, N_HALF], U8))
+            nc.vector.quantize_mx(
+                out=w3_codes[u][:].bitcast(FP8X4), scales=w3_sc[u][:], in_=w3_bf[:].rearrange("p n j -> p (n j)")
+            )
+
+        for u in range(2):
+            picks = idx2[:, u * (M_HALF // 16) : (u + 1) * (M_HALF // 16)]
+            bounded = sbt(f"bounded{u}", [P, PACK, M_HALF], F32)
+            looked = sbt("looked" if u == 0 else "stage", [P, PACK, 2, M_HALF], F32)
+            for i in range(PACK):
+                gate = looked[:, i, 0, :]
+                hp = looked[:, i, 1, :]
+                nc.scalar.activation(
+                    out=gate, in_=h[i][:].indirect(picks), func=ACT.Sigmoid,
+                    bias=th_sb[:, i : i + 1], scale=sc_sb[:, i : i + 1],
+                )
+                nc.scalar.activation(out=hp, in_=h[i][:].indirect(picks), func=ACT.Copy)
+                nc.vector.tensor_tensor(bounded[:, i, :], gate, hp, ALU.min)
+            e_bf = sbt(f"e_bf{u}", [P, M_HALF, PACK], BF16)
+            nc.vector.tensor_tensor(
+                e_bf[:].rearrange("p (c k) i -> p c i k", k=4),
+                bounded[:].rearrange("p i (c k) -> p c i k", k=4),
+                gain_sb[:].unsqueeze(1).unsqueeze(3).to_broadcast([P, M_HALF // 4, PACK, 4]),
+                ALU.mult,
+            )
+            e_codes = sbt(f"e_codes{u}", [P, M_HALF], U32)
+            e_sc = sbt(f"e_sc{u}", [P, M_HALF], U8)
+            nc.vector.quantize_mx(
+                out=e_codes[:].bitcast(FP8X4), scales=e_sc[:], in_=e_bf[:].rearrange("p m i -> p (m i)")
+            )
+            cols = slice(u * M_HALF, (u + 1) * M_HALF)
+            for g in range(N // (2 * P)):
+                y3 = psum.tile([P, 2, M_HALF], F32, name=f"bank{3 * u + g}")
+                for t in range(2):
+                    wu, wt = divmod(2 * g + t, N_HALF // P)
+                    nc.tensor.matmul_mx(
+                        out=y3[:, t, :],
+                        lhsT=w3_codes[wu][:, P * wt : P * (wt + 1)].bitcast(FP8X4),
+                        lhsT_scale=w3_sc[wu][:, P * wt : P * (wt + 1)],
+                        rhs=e_codes[:].bitcast(FP8X4),
+                        rhs_scale=e_sc[:],
+                        start=True,
+                        stop=True,
+                    )
+                nc.vector.tensor_tensor(score[g][:, :, cols], y3[:], score[g][:, :, cols], ALU.max)
+                nc.sync.dma_start(out_rows[g][:, :, cols], score[g][:, :, cols])

@@ -23,7 +23,8 @@ BANK = 512
 S_HALVES = S // BANK
 M_HALF = M // 2
 N_HALF = N // 2
-SHIFT_ROWS = 112
+WHOLE_LOOKS = 2
+PARKED = (4, 68, 112)
 
 
 def tile_list_arm_leak_scores_kernel(
@@ -37,23 +38,71 @@ def tile_list_arm_leak_scores_kernel(
         def sbt(name, shape, dtype):
             return sb.tile(shape, dtype, name=name, align_bytes=64)
 
+        tab_sc = sbt("tab_sc", [P, T], U8)
+        nc.vector.memset(tab_sc[:].bitcast(I32), 0)
+        w2_sc_raw = sbt("w2_sc_raw", [P, PASSES, H], U8)
+        nc.vector.memset(w2_sc_raw[:].bitcast(I32), 0)
+        v_sc = []
+        for a in range(PASSES):
+            v_sc.append(sbt(f"v_sc{a}", [P, S], U8))
+            nc.gpsimd.memset(v_sc[a][:].bitcast(I32), 0)
+
         idx = sbt("idx", [P, S // 16], U16)
         nc.sync.dma_start(idx[:], offs)
-        w2_raw = sbt("w2_raw", [P, PASSES, 2 * H], U8)
-        nc.sync.dma_start(w2_raw[:].bitcast(I32), w2_words.rearrange("a p c -> p a c").bitcast(I32))
-        tab = []
+        tab = [sbt(f"tab{a}", [P, T], U32) for a in range(PASSES)]
+
+        def load_tab(a, cols=slice(0, T)):
+            words = tab_words[a].rearrange("p t i -> p (t i)").bitcast(I32)
+            nc.sync.dma_start(tab[a][:, cols].bitcast(I32), words[:, cols])
+
+        load_tab(0, slice(0, T // 2))
         for a in range(PASSES):
-            tab.append(sbt(f"tab{a}", [P, T], U32))
-            nc.sync.dma_start(tab[a][:].bitcast(I32), tab_words[a].rearrange("p t i -> p (t i)").bitcast(I32))
+            nc.sync.dma_start(tab_sc[PARKED[a] : PARKED[a] + 16, :].bitcast(I32), tab_scales[a].bitcast(I32))
+        w2_raw = sbt("w2_raw", [P, PASSES, H], U16)
+        nc.sync.dma_start(w2_raw[:].bitcast(I32), w2_words.rearrange("a p c -> p a c").bitcast(I32))
+        load_tab(0, slice(T // 2, T))
+        for q in range(4):
+            nc.sync.dma_start(
+                w2_sc_raw[32 * q : 32 * q + 4, :, :].bitcast(I32),
+                w2_scales[:, 4 * q : 4 * q + 4, :].rearrange("a r c -> r a c").bitcast(I32),
+            )
+        load_tab(1, slice(0, 3 * T // 4))
+
+        picked_sc = sbt("picked_sc", [P, S], U8)
+        nc.vector.tensor_copy(picked_sc[:], tab_sc[:].indirect(idx[:]))
+        w2_codes = sbt("w2_codes", [P, PASSES, H], U16)
+        nc.vector.tensor_copy(
+            w2_codes[:].rearrange("p a (i m) -> p a i m", i=PACK),
+            w2_raw[:].rearrange("p a (m i) -> p a i m", i=PACK),
+        )
+        w2_sc = sbt("w2_sc", [P, PASSES, H], U8)
+        for a in range(PASSES):
+            nc.vector.tensor_copy(
+                w2_sc[:, a, :].rearrange("p (i m) -> p i m", i=PACK),
+                w2_sc_raw[:, a, :].rearrange("p (m i) -> p i m", i=PACK),
+            )
+
+        def place_scales(a):
+            for q in range(4):
+                rows = slice(PARKED[a] + 4 * q, PARKED[a] + 4 * q + 4)
+                nc.sync.dma_start(v_sc[a][32 * q : 32 * q + 4, :].bitcast(I32), picked_sc[rows, :].bitcast(I32))
+
+        place_scales(0)
+        load_tab(1, slice(3 * T // 4, T))
+        load_tab(2, slice(0, 3 * T // 8))
+        place_scales(1)
+        load_tab(2, slice(3 * T // 8, T))
+        place_scales(2)
 
         def load_rows(name, vec):
             t = sbt(name, [P, PACK], F32)
-            nc.scalar.dma_start(t[:], vec.rearrange("(p i) -> p i", i=PACK))
+            nc.gpsimd.dma_start(t[:], vec.rearrange("(p i) -> p i", i=PACK))
             return t
 
-        idx2 = sbt("idx2", [P, M // 16], U16)
-        nc.sync.dma_start(idx2[:], offs2)
         b2_sb = load_rows("b2_sb", b2)
+        sc_sb = load_rows("sc_sb", sc)
+        th_sb = load_rows("th_sb", th)
+        gain_sb = load_rows("gain_sb", gain)
         w1_rows = w1.rearrange("(a p j) c -> a p j c", p=P, j=PACK)
         w1_raw = []
         for a in range(PASSES - 1):
@@ -63,9 +112,8 @@ def tile_list_arm_leak_scores_kernel(
         for u in range(2):
             w1_last.append(sbt(f"w1_last{u}", [P, PACK, H // 2], F32))
             nc.sync.dma_start(w1_last[u][:], w1_rows[PASSES - 1][:, :, u * (H // 2) : (u + 1) * (H // 2)])
-        sc_sb = load_rows("sc_sb", sc)
-        th_sb = load_rows("th_sb", th)
-        gain_sb = load_rows("gain_sb", gain)
+        idx2 = sbt("idx2", [P, M // 16], U16)
+        nc.sync.dma_start(idx2[:], offs2)
         w3_rows = w3.rearrange("(p j) n -> p j n", j=PACK)
         w3_raw = []
         for u in range(2):
@@ -77,43 +125,6 @@ def tile_list_arm_leak_scores_kernel(
         for g in range(N // (2 * P)):
             score.append(sbt(f"score{g}", [P, 2, M], F32))
             nc.sync.dma_start(score[g][:], low_rows[g])
-
-        tab_sc = sbt("tab_sc", [P, T], U8)
-        nc.gpsimd.memset(tab_sc[:].bitcast(I32), 0)
-        for q in range(4):
-            nc.gpsimd.dma_start(
-                tab_sc[32 * q : 32 * q + 4 * PASSES, :].bitcast(I32), tab_scales[:, 4 * q : 4 * q + 4, :].bitcast(I32)
-            )
-        w2_sc_raw = sbt("w2_sc_raw", [P, PASSES, H], U8)
-        nc.gpsimd.memset(w2_sc_raw[:].bitcast(I32), 0)
-        for q in range(4):
-            nc.gpsimd.dma_start(
-                w2_sc_raw[32 * q : 32 * q + 4, :, :].bitcast(I32),
-                w2_scales[:, 4 * q : 4 * q + 4, :].rearrange("a r c -> r a c").bitcast(I32),
-            )
-        v_sc_low = {}
-        for a in range(1, PASSES):
-            v_sc_low[a] = sbt(f"v_sc_low{a}", [P, S], U8)
-            nc.gpsimd.memset(v_sc_low[a][:].bitcast(I32), 0)
-
-        w2_codes = sbt("w2_codes", [P, PASSES, 2 * H], U8)
-        nc.vector.tensor_copy(
-            w2_codes[:].rearrange("p a (i m b) -> p a m i b", i=PACK, b=2),
-            w2_raw[:].rearrange("p a (m i b) -> p a m i b", i=PACK, b=2),
-        )
-        w2_sc = sbt("w2_sc", [P, PASSES, H], U8)
-        nc.vector.tensor_copy(
-            w2_sc[:].rearrange("p a (i m) -> p a m i", i=PACK),
-            w2_sc_raw[:].rearrange("p a (m i) -> p a m i", i=PACK),
-        )
-
-        v_sc = sbt("v_sc", [P, S], U8)
-        nc.vector.tensor_copy(v_sc[:], tab_sc[:].indirect(idx[:]))
-        for a in range(1, PASSES):
-            nc.gpsimd.dma_start(
-                v_sc_low[a][0:SHIFT_ROWS, :].bitcast(I32), v_sc[4 * a : 4 * a + SHIFT_ROWS, :].bitcast(I32)
-            )
-        v_sc_low[0] = v_sc
 
         y2 = {}
         v_codes = {}
@@ -128,10 +139,10 @@ def tile_list_arm_leak_scores_kernel(
                         y2[i, s] = psum.tile([P, BANK], F32, name=f"bank{S_HALVES * i + s}")
                     nc.tensor.matmul_mx(
                         out=y2[i, s][:],
-                        lhsT=w2_codes[:, a, 2 * P * i : 2 * P * (i + 1)].bitcast(FP4X4),
+                        lhsT=w2_codes[:, a, P * i : P * (i + 1)].bitcast(FP4X4),
                         lhsT_scale=w2_sc[:, a, P * i : P * (i + 1)],
                         rhs=v_codes[a, s][:].bitcast(FP8X4),
-                        rhs_scale=v_sc_low[a][:, s * BANK : (s + 1) * BANK],
+                        rhs_scale=v_sc[a][:, s * BANK : (s + 1) * BANK],
                         start=(a == 0),
                         stop=(a == PASSES - 1),
                     )
@@ -149,19 +160,19 @@ def tile_list_arm_leak_scores_kernel(
         w1_sc = [sbt(f"w1_sc{a}", [P, H], U8) for a in range(PASSES)]
         for a in range(PASSES - 1):
             nc.vector.tensor_copy(
-                w1_bf[a][:].rearrange("p i m j -> p m j i"), w1_raw[a][:].rearrange("p j (m i) -> p m j i", i=PACK)
+                w1_bf[a][:].rearrange("p (x y) m j -> p x m j y", y=2), w1_raw[a][:].rearrange("p j (m x y) -> p x m j y", x=2, y=2)
             )
             nc.vector.quantize_mx(
                 out=w1_codes[a][:].bitcast(FP8X4), scales=w1_sc[a][:], in_=w1_bf[a][:].rearrange("p i m j -> p (i m j)")
             )
         last = PASSES - 1
-        nc.scalar.copy(
-            w1_bf[last][:, :, 0 : P // 2, :].rearrange("p i m j -> p m j i"),
-            w1_last[0][:].rearrange("p j (m i) -> p m j i", i=PACK),
+        nc.vector.tensor_copy(
+            w1_bf[last][:, :, 0 : P // 2, :].rearrange("p (x y) m j -> p x m j y", y=2),
+            w1_last[0][:].rearrange("p j (m x y) -> p x m j y", x=2, y=2),
         )
         nc.vector.tensor_copy(
-            w1_bf[last][:, :, P // 2 : P, :].rearrange("p i m j -> p m j i"),
-            w1_last[1][:].rearrange("p j (m i) -> p m j i", i=PACK),
+            w1_bf[last][:, :, P // 2 : P, :].rearrange("p (x y) m j -> p x m j y", y=2),
+            w1_last[1][:].rearrange("p j (m x y) -> p x m j y", x=2, y=2),
         )
 
         y1 = {}
@@ -172,7 +183,7 @@ def tile_list_arm_leak_scores_kernel(
                 lhsT=w1_codes[a][:, P * i : P * (i + 1)].bitcast(FP8X4),
                 lhsT_scale=w1_sc[a][:, P * i : P * (i + 1)],
                 rhs=v_codes[a, s][:].bitcast(FP8X4),
-                rhs_scale=v_sc[4 * a : P, s * BANK : (s + 1) * BANK],
+                rhs_scale=v_sc[a][:, s * BANK : (s + 1) * BANK],
                 start=(a == 0),
                 stop=(a == last),
             )
@@ -195,57 +206,65 @@ def tile_list_arm_leak_scores_kernel(
                 cols = slice(s * BANK, (s + 1) * BANK)
                 nc.vector.tensor_tensor(h[i][:, cols], y1[i, s][:], bent[:, i, cols], ALU.add)
 
-        w3_codes = []
-        w3_sc = []
+        w3_bf = sbt("w3_bf", [P, N, PACK], BF16)
         for u in range(2):
-            w3_bf = sbt(f"w3_bf{u}", [P, N_HALF, PACK], BF16)
             nc.gpsimd.tensor_scalar(
-                w3_bf[:], w3_raw[u][:].rearrange("p j n -> p n j"), 1.0, 0.0, ALU.mult, ALU.add
+                w3_bf[:, u * N_HALF : (u + 1) * N_HALF, :], w3_raw[u][:].rearrange("p j n -> p n j"),
+                1.0, 0.0, ALU.mult, ALU.add,
             )
-            w3_codes.append(sbt(f"w3_codes{u}", [P, N_HALF], U32))
-            w3_sc.append(sbt(f"w3_sc{u}", [P, N_HALF], U8))
+        w3_codes = sbt("w3_codes", [P, N], U32)
+        w3_sc = sbt("w3_sc", [P, N], U8)
+        for ns in (slice(0, 512), slice(512, N)):
             nc.vector.quantize_mx(
-                out=w3_codes[u][:].bitcast(FP8X4), scales=w3_sc[u][:], in_=w3_bf[:].rearrange("p n j -> p (n j)")
+                out=w3_codes[:, ns].bitcast(FP8X4), scales=w3_sc[:, ns], in_=w3_bf[:, ns, :].rearrange("p n j -> p (n j)")
             )
 
+        bounded = sbt("bounded", [P, PACK, M], F32)
+        e_rows = sbt("e_rows", [P, PACK, M], BF16)
+
+        def look(i, cols, gate, hp):
+            picks = idx2[:, cols.start // 16 : cols.stop // 16]
+            nc.scalar.activation(
+                out=gate, in_=h[i][:].indirect(picks), func=ACT.Sigmoid,
+                bias=th_sb[:, i : i + 1], scale=sc_sb[:, i : i + 1],
+            )
+            nc.scalar.activation(out=hp, in_=h[i][:].indirect(picks), func=ACT.Copy)
+            nc.vector.tensor_tensor(bounded[:, i, cols], gate, hp, ALU.min)
+            nc.vector.tensor_scalar(e_rows[:, i, cols], bounded[:, i, cols], gain_sb[:, i : i + 1], None, ALU.mult)
+
+        whole = sbt("whole", [P, WHOLE_LOOKS, 2, M], F32)
+        for i in range(WHOLE_LOOKS):
+            look(i, slice(0, M), whole[:, i, 0, :], whole[:, i, 1, :])
+        y3 = {}
         for u in range(2):
-            picks = idx2[:, u * (M_HALF // 16) : (u + 1) * (M_HALF // 16)]
-            bounded = sbt(f"bounded{u}", [P, PACK, M_HALF], F32)
-            looked = sbt("looked" if u == 0 else "stage", [P, PACK, 2, M_HALF], F32)
-            for i in range(PACK):
-                gate = looked[:, i, 0, :]
-                hp = looked[:, i, 1, :]
-                nc.scalar.activation(
-                    out=gate, in_=h[i][:].indirect(picks), func=ACT.Sigmoid,
-                    bias=th_sb[:, i : i + 1], scale=sc_sb[:, i : i + 1],
-                )
-                nc.scalar.activation(out=hp, in_=h[i][:].indirect(picks), func=ACT.Copy)
-                nc.vector.tensor_tensor(bounded[:, i, :], gate, hp, ALU.min)
+            cols = slice(u * M_HALF, (u + 1) * M_HALF)
+            halved = sbt("halved" if u == 0 else "stage", [P, PACK - WHOLE_LOOKS, 2, M_HALF], F32)
+            for i in range(WHOLE_LOOKS, PACK):
+                look(i, cols, halved[:, i - WHOLE_LOOKS, 0, :], halved[:, i - WHOLE_LOOKS, 1, :])
             e_bf = sbt(f"e_bf{u}", [P, M_HALF, PACK], BF16)
-            nc.vector.tensor_tensor(
-                e_bf[:].rearrange("p (c k) i -> p c i k", k=4),
-                bounded[:].rearrange("p i (c k) -> p c i k", k=4),
-                gain_sb[:].unsqueeze(1).unsqueeze(3).to_broadcast([P, M_HALF // 4, PACK, 4]),
-                ALU.mult,
+            nc.vector.tensor_copy(
+                e_bf[:].rearrange("p (c k) i -> p c i k", k=4), e_rows[:, :, cols].rearrange("p i (c k) -> p c i k", k=4)
             )
             e_codes = sbt(f"e_codes{u}", [P, M_HALF], U32)
             e_sc = sbt(f"e_sc{u}", [P, M_HALF], U8)
             nc.vector.quantize_mx(
                 out=e_codes[:].bitcast(FP8X4), scales=e_sc[:], in_=e_bf[:].rearrange("p m i -> p (m i)")
             )
-            cols = slice(u * M_HALF, (u + 1) * M_HALF)
             for g in range(N // (2 * P)):
-                y3 = psum.tile([P, 2, M_HALF], F32, name=f"bank{3 * u + g}")
+                y3[u, g] = psum.tile([P, 2, M_HALF], F32, name=f"bank{3 * u + g}")
                 for t in range(2):
-                    wu, wt = divmod(2 * g + t, N_HALF // P)
+                    ns = slice(P * (2 * g + t), P * (2 * g + t + 1))
                     nc.tensor.matmul_mx(
-                        out=y3[:, t, :],
-                        lhsT=w3_codes[wu][:, P * wt : P * (wt + 1)].bitcast(FP8X4),
-                        lhsT_scale=w3_sc[wu][:, P * wt : P * (wt + 1)],
+                        out=y3[u, g][:, t, :],
+                        lhsT=w3_codes[:, ns].bitcast(FP8X4),
+                        lhsT_scale=w3_sc[:, ns],
                         rhs=e_codes[:].bitcast(FP8X4),
                         rhs_scale=e_sc[:],
                         start=True,
                         stop=True,
                     )
-                nc.vector.tensor_tensor(score[g][:, :, cols], y3[:], score[g][:, :, cols], ALU.max)
+        for u in range(2):
+            cols = slice(u * M_HALF, (u + 1) * M_HALF)
+            for g in range(N // (2 * P)):
+                nc.vector.tensor_tensor(score[g][:, :, cols], y3[u, g][:], score[g][:, :, cols], ALU.max)
                 nc.sync.dma_start(out_rows[g][:, :, cols], score[g][:, :, cols])

@@ -22,7 +22,7 @@ PASSES = K // (P * PACK)
 BANK = 512
 S_HALVES = S // BANK
 M_HALF = M // 2
-N_HALF = N // 2
+N_PAIRS = N // (2 * P)
 WHOLE_LOOKS = 2
 PARKED = (4, 68, 112)
 
@@ -45,7 +45,7 @@ def tile_list_arm_leak_scores_kernel(
         v_sc = []
         for a in range(PASSES):
             v_sc.append(sbt(f"v_sc{a}", [P, S], U8))
-            nc.gpsimd.memset(v_sc[a][:].bitcast(I32), 0)
+            nc.vector.memset(v_sc[a][:].bitcast(I32), 0)
 
         idx = sbt("idx", [P, S // 16], U16)
         nc.sync.dma_start(idx[:], offs)
@@ -87,42 +87,42 @@ def tile_list_arm_leak_scores_kernel(
                 rows = slice(PARKED[a] + 4 * q, PARKED[a] + 4 * q + 4)
                 nc.sync.dma_start(v_sc[a][32 * q : 32 * q + 4, :].bitcast(I32), picked_sc[rows, :].bitcast(I32))
 
+        def load_rows(name, vec):
+            t = sbt(name, [P, PACK], F32)
+            nc.sync.dma_start(t[:], vec.rearrange("(p i) -> p i", i=PACK))
+            return t
+
         place_scales(0)
         load_tab(1, slice(3 * T // 4, T))
         load_tab(2, slice(0, 3 * T // 8))
         place_scales(1)
+        b2_sb = load_rows("b2_sb", b2)
         load_tab(2, slice(3 * T // 8, T))
         place_scales(2)
 
-        def load_rows(name, vec):
-            t = sbt(name, [P, PACK], F32)
-            nc.gpsimd.dma_start(t[:], vec.rearrange("(p i) -> p i", i=PACK))
-            return t
-
-        b2_sb = load_rows("b2_sb", b2)
-        sc_sb = load_rows("sc_sb", sc)
-        th_sb = load_rows("th_sb", th)
-        gain_sb = load_rows("gain_sb", gain)
         w1_rows = w1.rearrange("(a p j) c -> a p j c", p=P, j=PACK)
         w1_raw = []
         for a in range(PASSES - 1):
             w1_raw.append(sbt(f"w1_raw{a}", [P, PACK, H], F32))
             nc.sync.dma_start(w1_raw[a][:], w1_rows[a])
+        idx2 = sbt("idx2", [P, M // 16], U16)
+        nc.sync.dma_start(idx2[:], offs2)
+        sc_sb = load_rows("sc_sb", sc)
+        th_sb = load_rows("th_sb", th)
+        gain_sb = load_rows("gain_sb", gain)
         w1_last = []
         for u in range(2):
             w1_last.append(sbt(f"w1_last{u}", [P, PACK, H // 2], F32))
             nc.sync.dma_start(w1_last[u][:], w1_rows[PASSES - 1][:, :, u * (H // 2) : (u + 1) * (H // 2)])
-        idx2 = sbt("idx2", [P, M // 16], U16)
-        nc.sync.dma_start(idx2[:], offs2)
         w3_rows = w3.rearrange("(p j) n -> p j n", j=PACK)
         w3_raw = []
-        for u in range(2):
-            w3_raw.append(sbt(f"w3_raw{u}", [P, PACK, N_HALF], F32))
-            nc.sync.dma_start(w3_raw[u][:], w3_rows[:, :, u * N_HALF : (u + 1) * N_HALF])
+        for g in range(N_PAIRS):
+            w3_raw.append(sbt(f"w3_raw{g}", [P, PACK, 2 * P], F32))
+            nc.sync.dma_start(w3_raw[g][:], w3_rows[:, :, 2 * P * g : 2 * P * (g + 1)])
         low_rows = low.rearrange("(g t p) m -> g p t m", t=2, p=P)
         out_rows = out.rearrange("(g t p) m -> g p t m", t=2, p=P)
         score = []
-        for g in range(N // (2 * P)):
+        for g in range(N_PAIRS):
             score.append(sbt(f"score{g}", [P, 2, M], F32))
             nc.sync.dma_start(score[g][:], low_rows[g])
 
@@ -206,41 +206,49 @@ def tile_list_arm_leak_scores_kernel(
                 cols = slice(s * BANK, (s + 1) * BANK)
                 nc.vector.tensor_tensor(h[i][:, cols], y1[i, s][:], bent[:, i, cols], ALU.add)
 
-        w3_bf = sbt("w3_bf", [P, N, PACK], BF16)
-        for u in range(2):
-            nc.gpsimd.tensor_scalar(
-                w3_bf[:, u * N_HALF : (u + 1) * N_HALF, :], w3_raw[u][:].rearrange("p j n -> p n j"),
-                1.0, 0.0, ALU.mult, ALU.add,
-            )
         w3_codes = sbt("w3_codes", [P, N], U32)
         w3_sc = sbt("w3_sc", [P, N], U8)
-        for ns in (slice(0, 512), slice(512, N)):
-            nc.vector.quantize_mx(
-                out=w3_codes[:, ns].bitcast(FP8X4), scales=w3_sc[:, ns], in_=w3_bf[:, ns, :].rearrange("p n j -> p (n j)")
+        w3_early = sbt("w3_early", [P, 2, 2 * P, PACK], BF16)
+        for g in range(2):
+            nc.scalar.copy(
+                w3_early[:, g].rearrange("p (c k) j -> p c j k", k=4), w3_raw[g][:].rearrange("p j (c k) -> p c j k", k=4)
             )
+        w3_late = sbt("w3_late", [P, 2 * P, PACK], BF16)
+        nc.vector.tensor_copy(
+            w3_late[:].rearrange("p (c k) j -> p c j k", k=4), w3_raw[2][:].rearrange("p j (c k) -> p c j k", k=4)
+        )
+        nc.vector.quantize_mx(
+            out=w3_codes[:, 0 : 4 * P].bitcast(FP8X4), scales=w3_sc[:, 0 : 4 * P],
+            in_=w3_early[:].rearrange("p g n j -> p (g n j)"),
+        )
+        nc.vector.quantize_mx(
+            out=w3_codes[:, 4 * P : N].bitcast(FP8X4), scales=w3_sc[:, 4 * P : N],
+            in_=w3_late[:].rearrange("p n j -> p (n j)"),
+        )
 
-        bounded = sbt("bounded", [P, PACK, M], F32)
         e_rows = sbt("e_rows", [P, PACK, M], BF16)
 
-        def look(i, cols, gate, hp):
+        def look(i, cols, gate, hp, slot):
             picks = idx2[:, cols.start // 16 : cols.stop // 16]
             nc.scalar.activation(
                 out=gate, in_=h[i][:].indirect(picks), func=ACT.Sigmoid,
                 bias=th_sb[:, i : i + 1], scale=sc_sb[:, i : i + 1],
             )
             nc.scalar.activation(out=hp, in_=h[i][:].indirect(picks), func=ACT.Copy)
-            nc.vector.tensor_tensor(bounded[:, i, cols], gate, hp, ALU.min)
-            nc.vector.tensor_scalar(e_rows[:, i, cols], bounded[:, i, cols], gain_sb[:, i : i + 1], None, ALU.mult)
+            bounded = sbt(slot, [P, cols.stop - cols.start], F32)
+            nc.vector.tensor_tensor(bounded[:], gate, hp, ALU.min)
+            nc.vector.tensor_scalar(e_rows[:, i, cols], bounded[:], gain_sb[:, i : i + 1], None, ALU.mult)
 
         whole = sbt("whole", [P, WHOLE_LOOKS, 2, M], F32)
         for i in range(WHOLE_LOOKS):
-            look(i, slice(0, M), whole[:, i, 0, :], whole[:, i, 1, :])
+            look(i, slice(0, M), whole[:, i, 0, :], whole[:, i, 1, :], f"bounded{i}")
         y3 = {}
+        slots = ({2: "bounded2", 3: "bounded3"}, {2: "bounded3", 3: "e_bf0"})
         for u in range(2):
             cols = slice(u * M_HALF, (u + 1) * M_HALF)
             halved = sbt("halved" if u == 0 else "stage", [P, PACK - WHOLE_LOOKS, 2, M_HALF], F32)
             for i in range(WHOLE_LOOKS, PACK):
-                look(i, cols, halved[:, i - WHOLE_LOOKS, 0, :], halved[:, i - WHOLE_LOOKS, 1, :])
+                look(i, cols, halved[:, i - WHOLE_LOOKS, 0, :], halved[:, i - WHOLE_LOOKS, 1, :], slots[u][i])
             e_bf = sbt(f"e_bf{u}", [P, M_HALF, PACK], BF16)
             nc.vector.tensor_copy(
                 e_bf[:].rearrange("p (c k) i -> p c i k", k=4), e_rows[:, :, cols].rearrange("p i (c k) -> p c i k", k=4)
@@ -250,7 +258,7 @@ def tile_list_arm_leak_scores_kernel(
             nc.vector.quantize_mx(
                 out=e_codes[:].bitcast(FP8X4), scales=e_sc[:], in_=e_bf[:].rearrange("p m i -> p (m i)")
             )
-            for g in range(N // (2 * P)):
+            for g in range(N_PAIRS):
                 y3[u, g] = psum.tile([P, 2, M_HALF], F32, name=f"bank{3 * u + g}")
                 for t in range(2):
                     ns = slice(P * (2 * g + t), P * (2 * g + t + 1))
@@ -265,6 +273,6 @@ def tile_list_arm_leak_scores_kernel(
                     )
         for u in range(2):
             cols = slice(u * M_HALF, (u + 1) * M_HALF)
-            for g in range(N // (2 * P)):
+            for g in range(N_PAIRS):
                 nc.vector.tensor_tensor(score[g][:, :, cols], y3[u, g][:], score[g][:, :, cols], ALU.max)
                 nc.sync.dma_start(out_rows[g][:, :, cols], score[g][:, :, cols])

@@ -19,12 +19,22 @@ ALU = mybir.AluOpType
 P = 128
 PACK = 4
 PASSES = K // (P * PACK)
+LAST = PASSES - 1
+BLOCKS = 16
+QUADRANTS = 4
+GROUP = 16
 BANK = 512
 S_HALVES = S // BANK
 M_HALF = M // 2
+N_HALF = N // 2
 N_PAIRS = N // (2 * P)
-WHOLE_LOOKS = 2
+LINE = 4
+
 PARKED = (4, 68, 112)
+TAB_CUT = (T // 2, 3 * T // 4, 3 * T // 8)
+WHOLE_LOOKS = 2
+EARLY_SETS = 2
+W3_FIRST = 512
 
 
 def tile_list_arm_leak_scores_kernel(
@@ -47,26 +57,26 @@ def tile_list_arm_leak_scores_kernel(
             v_sc.append(sbt(f"v_sc{a}", [P, S], U8))
             nc.vector.memset(v_sc[a][:].bitcast(I32), 0)
 
-        idx = sbt("idx", [P, S // 16], U16)
+        idx = sbt("idx", [P, S // GROUP], U16)
         nc.sync.dma_start(idx[:], offs)
         tab = [sbt(f"tab{a}", [P, T], U32) for a in range(PASSES)]
 
-        def load_tab(a, cols=slice(0, T)):
+        def load_tab(a, first, end):
             words = tab_words[a].rearrange("p t i -> p (t i)").bitcast(I32)
-            nc.sync.dma_start(tab[a][:, cols].bitcast(I32), words[:, cols])
+            nc.sync.dma_start(tab[a][:, first:end].bitcast(I32), words[:, first:end])
 
-        load_tab(0, slice(0, T // 2))
+        load_tab(0, 0, TAB_CUT[0])
         for a in range(PASSES):
-            nc.sync.dma_start(tab_sc[PARKED[a] : PARKED[a] + 16, :].bitcast(I32), tab_scales[a].bitcast(I32))
+            nc.sync.dma_start(tab_sc[PARKED[a] : PARKED[a] + BLOCKS, :].bitcast(I32), tab_scales[a].bitcast(I32))
         w2_raw = sbt("w2_raw", [P, PASSES, H], U16)
         nc.sync.dma_start(w2_raw[:].bitcast(I32), w2_words.rearrange("a p c -> p a c").bitcast(I32))
-        load_tab(0, slice(T // 2, T))
-        for q in range(4):
+        load_tab(0, TAB_CUT[0], T)
+        for q in range(QUADRANTS):
             nc.sync.dma_start(
                 w2_sc_raw[32 * q : 32 * q + 4, :, :].bitcast(I32),
                 w2_scales[:, 4 * q : 4 * q + 4, :].rearrange("a r c -> r a c").bitcast(I32),
             )
-        load_tab(1, slice(0, 3 * T // 4))
+        load_tab(1, 0, TAB_CUT[1])
 
         picked_sc = sbt("picked_sc", [P, S], U8)
         nc.vector.tensor_copy(picked_sc[:], tab_sc[:].indirect(idx[:]))
@@ -83,42 +93,42 @@ def tile_list_arm_leak_scores_kernel(
             )
 
         def place_scales(a):
-            for q in range(4):
+            for q in range(QUADRANTS):
                 rows = slice(PARKED[a] + 4 * q, PARKED[a] + 4 * q + 4)
                 nc.sync.dma_start(v_sc[a][32 * q : 32 * q + 4, :].bitcast(I32), picked_sc[rows, :].bitcast(I32))
 
         def load_rows(name, vec):
-            t = sbt(name, [P, PACK], F32)
-            nc.sync.dma_start(t[:], vec.rearrange("(p i) -> p i", i=PACK))
-            return t
+            by_set = sbt(name, [P, PACK], F32)
+            nc.sync.dma_start(by_set[:], vec.rearrange("(p i) -> p i", i=PACK))
+            return by_set
 
         place_scales(0)
-        load_tab(1, slice(3 * T // 4, T))
-        load_tab(2, slice(0, 3 * T // 8))
+        load_tab(1, TAB_CUT[1], T)
+        load_tab(2, 0, TAB_CUT[2])
         place_scales(1)
         b2_sb = load_rows("b2_sb", b2)
-        load_tab(2, slice(3 * T // 8, T))
+        load_tab(2, TAB_CUT[2], T)
         place_scales(2)
 
         w1_rows = w1.rearrange("(a p j) c -> a p j c", p=P, j=PACK)
         w1_raw = []
-        for a in range(PASSES - 1):
+        for a in range(LAST):
             w1_raw.append(sbt(f"w1_raw{a}", [P, PACK, H], F32))
             nc.sync.dma_start(w1_raw[a][:], w1_rows[a])
-        idx2 = sbt("idx2", [P, M // 16], U16)
+        w1_last = []
+        for half in range(2):
+            w1_last.append(sbt(f"w1_last{half}", [P, PACK, H // 2], F32))
+            nc.sync.dma_start(w1_last[half][:], w1_rows[LAST][:, :, half * (H // 2) : (half + 1) * (H // 2)])
+        idx2 = sbt("idx2", [P, M // GROUP], U16)
         nc.sync.dma_start(idx2[:], offs2)
         sc_sb = load_rows("sc_sb", sc)
         th_sb = load_rows("th_sb", th)
         gain_sb = load_rows("gain_sb", gain)
-        w1_last = []
-        for u in range(2):
-            w1_last.append(sbt(f"w1_last{u}", [P, PACK, H // 2], F32))
-            nc.sync.dma_start(w1_last[u][:], w1_rows[PASSES - 1][:, :, u * (H // 2) : (u + 1) * (H // 2)])
         w3_rows = w3.rearrange("(p j) n -> p j n", j=PACK)
         w3_raw = []
-        for g in range(N_PAIRS):
-            w3_raw.append(sbt(f"w3_raw{g}", [P, PACK, 2 * P], F32))
-            nc.sync.dma_start(w3_raw[g][:], w3_rows[:, :, 2 * P * g : 2 * P * (g + 1)])
+        for half in range(2):
+            w3_raw.append(sbt(f"w3_raw{half}", [P, PACK, N_HALF], F32))
+            nc.sync.dma_start(w3_raw[half][:], w3_rows[:, :, half * N_HALF : (half + 1) * N_HALF])
         low_rows = low.rearrange("(g t p) m -> g p t m", t=2, p=P)
         out_rows = out.rearrange("(g t p) m -> g p t m", t=2, p=P)
         score = []
@@ -132,7 +142,7 @@ def tile_list_arm_leak_scores_kernel(
             for s in range(S_HALVES):
                 v_codes[a, s] = sbt(f"v_codes{a}_{s}", [P, BANK], U32)
                 nc.vector.tensor_copy(
-                    v_codes[a, s][:], tab[a][:].indirect(idx[:, s * (BANK // 16) : (s + 1) * (BANK // 16)])
+                    v_codes[a, s][:], tab[a][:].indirect(idx[:, s * (BANK // GROUP) : (s + 1) * (BANK // GROUP)])
                 )
                 for i in range(PACK):
                     if a == 0:
@@ -144,40 +154,42 @@ def tile_list_arm_leak_scores_kernel(
                         rhs=v_codes[a, s][:].bitcast(FP8X4),
                         rhs_scale=v_sc[a][:, s * BANK : (s + 1) * BANK],
                         start=(a == 0),
-                        stop=(a == PASSES - 1),
+                        stop=(a == LAST),
                     )
 
         h = [sbt(f"h{i}", [P, S], F32) for i in range(PACK)]
-        bent = sbt("stage", [P, PACK, S], F32)
+        bent = sbt("bent", [P, PACK, S], F32)
         for s in range(S_HALVES):
             for i in range(PACK):
                 nc.scalar.activation(
                     out=bent[:, i, s * BANK : (s + 1) * BANK], in_=y2[i, s][:], func=ACT.Tanh, bias=b2_sb[:, i : i + 1]
                 )
 
-        w1_bf = [sbt(f"w1_bf{a}", [P, PACK, P, PACK], BF16) for a in range(PASSES)]
+        w1_bf = [sbt(f"w1_bf{a}", [P, PACK, P, PACK], BF16) for a in range(LAST)]
         w1_codes = [sbt(f"w1_codes{a}", [P, H], U32) for a in range(PASSES)]
         w1_sc = [sbt(f"w1_sc{a}", [P, H], U8) for a in range(PASSES)]
-        for a in range(PASSES - 1):
+        for a in range(LAST):
             nc.vector.tensor_copy(
-                w1_bf[a][:].rearrange("p (x y) m j -> p x m j y", y=2), w1_raw[a][:].rearrange("p j (m x y) -> p x m j y", x=2, y=2)
+                w1_bf[a][:].rearrange("p (x y) m j -> p x m j y", y=2),
+                w1_raw[a][:].rearrange("p j (m x y) -> p x m j y", x=2, y=2),
             )
             nc.vector.quantize_mx(
                 out=w1_codes[a][:].bitcast(FP8X4), scales=w1_sc[a][:], in_=w1_bf[a][:].rearrange("p i m j -> p (i m j)")
             )
-        last = PASSES - 1
-        nc.vector.tensor_copy(
-            w1_bf[last][:, :, 0 : P // 2, :].rearrange("p (x y) m j -> p x m j y", y=2),
-            w1_last[0][:].rearrange("p j (m x y) -> p x m j y", x=2, y=2),
-        )
-        nc.vector.tensor_copy(
-            w1_bf[last][:, :, P // 2 : P, :].rearrange("p (x y) m j -> p x m j y", y=2),
-            w1_last[1][:].rearrange("p j (m x y) -> p x m j y", x=2, y=2),
-        )
+        w1_pair = [sbt(f"w1_pair{x}", [P, 2, P, PACK], BF16) for x in range(2)]
+
+        def cast_last(x, half):
+            nc.vector.tensor_copy(
+                w1_pair[x][:, :, half * (P // 2) : (half + 1) * (P // 2), :].rearrange("p y m j -> p m j y"),
+                w1_last[half][:].rearrange("p j (m i) -> p m j i", i=PACK)[:, :, :, 2 * x : 2 * x + 2],
+            )
+
+        for x in range(2):
+            cast_last(x, 0)
 
         y1 = {}
 
-        def y1_pass(i, s, a):
+        def y1_pass(i, s, a, stop):
             nc.tensor.matmul_mx(
                 out=y1[i, s][:],
                 lhsT=w1_codes[a][:, P * i : P * (i + 1)].bitcast(FP8X4),
@@ -185,73 +197,87 @@ def tile_list_arm_leak_scores_kernel(
                 rhs=v_codes[a, s][:].bitcast(FP8X4),
                 rhs_scale=v_sc[a][:, s * BANK : (s + 1) * BANK],
                 start=(a == 0),
-                stop=(a == last),
+                stop=stop,
             )
 
         for s in range(S_HALVES):
             for i in range(PACK):
                 y1[i, s] = psum.tile([P, BANK], F32, name=f"bank{S_HALVES * i + s}")
-                y1_pass(i, s, 0)
-        for i in range(PACK):
+                y1_pass(i, s, 0, False)
+        for x in range(2):
+            cast_last(x, 1)
             nc.vector.quantize_mx(
-                out=w1_codes[last][:, P * i : P * (i + 1)].bitcast(FP8X4),
-                scales=w1_sc[last][:, P * i : P * (i + 1)],
-                in_=w1_bf[last][:, i, :, :].rearrange("p m j -> p (m j)"),
+                out=w1_codes[LAST][:, 2 * P * x : 2 * P * (x + 1)].bitcast(FP8X4),
+                scales=w1_sc[LAST][:, 2 * P * x : 2 * P * (x + 1)],
+                in_=w1_pair[x][:].rearrange("p y m j -> p (y m j)"),
             )
         for i in range(PACK):
-            for a in range(1, PASSES):
-                for s in range(S_HALVES):
-                    y1_pass(i, s, a)
+            order = (LAST - 1, LAST) if i < EARLY_SETS else (LAST, LAST - 1)
             for s in range(S_HALVES):
-                cols = slice(s * BANK, (s + 1) * BANK)
-                nc.vector.tensor_tensor(h[i][:, cols], y1[i, s][:], bent[:, i, cols], ALU.add)
+                for a in order:
+                    y1_pass(i, s, a, a == order[-1])
+            for s in range(S_HALVES):
+                s_cols = slice(s * BANK, (s + 1) * BANK)
+                nc.vector.tensor_tensor(h[i][:, s_cols], y1[i, s][:], bent[:, i, s_cols], ALU.add)
 
+        w3_bf = sbt("w3_bf", [P, N, PACK], BF16)
+        for half in range(2):
+            nc.gpsimd.tensor_scalar(
+                w3_bf[:, half * N_HALF : (half + 1) * N_HALF, :],
+                w3_raw[half][:].rearrange("p j n -> p n j"),
+                1.0,
+                0.0,
+                ALU.mult,
+                ALU.add,
+            )
         w3_codes = sbt("w3_codes", [P, N], U32)
         w3_sc = sbt("w3_sc", [P, N], U8)
-        w3_early = sbt("w3_early", [P, 2, 2 * P, PACK], BF16)
-        for g in range(2):
-            nc.scalar.copy(
-                w3_early[:, g].rearrange("p (c k) j -> p c j k", k=4), w3_raw[g][:].rearrange("p j (c k) -> p c j k", k=4)
+        for ns in (slice(0, W3_FIRST), slice(W3_FIRST, N)):
+            nc.vector.quantize_mx(
+                out=w3_codes[:, ns].bitcast(FP8X4),
+                scales=w3_sc[:, ns],
+                in_=w3_bf[:, ns, :].rearrange("p n j -> p (n j)"),
             )
-        w3_late = sbt("w3_late", [P, 2 * P, PACK], BF16)
-        nc.vector.tensor_copy(
-            w3_late[:].rearrange("p (c k) j -> p c j k", k=4), w3_raw[2][:].rearrange("p j (c k) -> p c j k", k=4)
-        )
-        nc.vector.quantize_mx(
-            out=w3_codes[:, 0 : 4 * P].bitcast(FP8X4), scales=w3_sc[:, 0 : 4 * P],
-            in_=w3_early[:].rearrange("p g n j -> p (g n j)"),
-        )
-        nc.vector.quantize_mx(
-            out=w3_codes[:, 4 * P : N].bitcast(FP8X4), scales=w3_sc[:, 4 * P : N],
-            in_=w3_late[:].rearrange("p n j -> p (n j)"),
-        )
 
         e_rows = sbt("e_rows", [P, PACK, M], BF16)
 
-        def look(i, cols, gate, hp, slot):
-            picks = idx2[:, cols.start // 16 : cols.stop // 16]
+        def look(i, m_cols, gate, hp, buffer, gain_on_scalar):
+            picks = idx2[:, m_cols.start // GROUP : m_cols.stop // GROUP]
             nc.scalar.activation(
-                out=gate, in_=h[i][:].indirect(picks), func=ACT.Sigmoid,
-                bias=th_sb[:, i : i + 1], scale=sc_sb[:, i : i + 1],
+                out=gate,
+                in_=h[i][:].indirect(picks),
+                func=ACT.Sigmoid,
+                bias=th_sb[:, i : i + 1],
+                scale=sc_sb[:, i : i + 1],
             )
             nc.scalar.activation(out=hp, in_=h[i][:].indirect(picks), func=ACT.Copy)
-            bounded = sbt(slot, [P, cols.stop - cols.start], F32)
+            bounded = sbt(buffer, [P, m_cols.stop - m_cols.start], F32)
             nc.vector.tensor_tensor(bounded[:], gate, hp, ALU.min)
-            nc.vector.tensor_scalar(e_rows[:, i, cols], bounded[:], gain_sb[:, i : i + 1], None, ALU.mult)
+            if gain_on_scalar:
+                nc.scalar.activation(
+                    out=e_rows[:, i, m_cols], in_=bounded[:], func=ACT.Copy, scale=gain_sb[:, i : i + 1]
+                )
+            else:
+                nc.vector.tensor_scalar(e_rows[:, i, m_cols], bounded[:], gain_sb[:, i : i + 1], None, ALU.mult)
 
         whole = sbt("whole", [P, WHOLE_LOOKS, 2, M], F32)
         for i in range(WHOLE_LOOKS):
-            look(i, slice(0, M), whole[:, i, 0, :], whole[:, i, 1, :], f"bounded{i}")
+            look(i, slice(0, M), whole[:, i, 0, :], whole[:, i, 1, :], f"bounded{i}", False)
+
+        looked_buffer = ("halved", "bent")
+        bounded_buffer = (("bounded2", "bounded3"), ("bounded3", "e_bf0"))
         y3 = {}
-        slots = ({2: "bounded2", 3: "bounded3"}, {2: "bounded3", 3: "e_bf0"})
         for u in range(2):
-            cols = slice(u * M_HALF, (u + 1) * M_HALF)
-            halved = sbt("halved" if u == 0 else "stage", [P, PACK - WHOLE_LOOKS, 2, M_HALF], F32)
-            for i in range(WHOLE_LOOKS, PACK):
-                look(i, cols, halved[:, i - WHOLE_LOOKS, 0, :], halved[:, i - WHOLE_LOOKS, 1, :], slots[u][i])
+            m_cols = slice(u * M_HALF, (u + 1) * M_HALF)
+            looked = sbt(looked_buffer[u], [P, PACK - WHOLE_LOOKS, 2, M_HALF], F32)
+            for late, i in enumerate(range(WHOLE_LOOKS, PACK)):
+                very_last = u == 1 and i == PACK - 1
+                look(i, m_cols, looked[:, late, 0, :], looked[:, late, 1, :], bounded_buffer[u][late], very_last)
             e_bf = sbt(f"e_bf{u}", [P, M_HALF, PACK], BF16)
-            nc.vector.tensor_copy(
-                e_bf[:].rearrange("p (c k) i -> p c i k", k=4), e_rows[:, :, cols].rearrange("p i (c k) -> p c i k", k=4)
+            interleave = nc.vector.tensor_copy if u == 0 else nc.scalar.copy
+            interleave(
+                e_bf[:].rearrange("p (c k) i -> p c i k", k=LINE),
+                e_rows[:, :, m_cols].rearrange("p i (c k) -> p c i k", k=LINE),
             )
             e_codes = sbt(f"e_codes{u}", [P, M_HALF], U32)
             e_sc = sbt(f"e_sc{u}", [P, M_HALF], U8)
@@ -259,7 +285,7 @@ def tile_list_arm_leak_scores_kernel(
                 out=e_codes[:].bitcast(FP8X4), scales=e_sc[:], in_=e_bf[:].rearrange("p m i -> p (m i)")
             )
             for g in range(N_PAIRS):
-                y3[u, g] = psum.tile([P, 2, M_HALF], F32, name=f"bank{3 * u + g}")
+                y3[u, g] = psum.tile([P, 2, M_HALF], F32, name=f"bank{N_PAIRS * u + g}")
                 for t in range(2):
                     ns = slice(P * (2 * g + t), P * (2 * g + t + 1))
                     nc.tensor.matmul_mx(
@@ -271,8 +297,13 @@ def tile_list_arm_leak_scores_kernel(
                         start=True,
                         stop=True,
                     )
+
         for u in range(2):
-            cols = slice(u * M_HALF, (u + 1) * M_HALF)
+            m_cols = slice(u * M_HALF, (u + 1) * M_HALF)
             for g in range(N_PAIRS):
-                nc.vector.tensor_tensor(score[g][:, :, cols], y3[u, g][:], score[g][:, :, cols], ALU.max)
-                nc.sync.dma_start(out_rows[g][:, :, cols], score[g][:, :, cols])
+                last_bank = u == 1 and g == N_PAIRS - 1
+                for ts in (slice(0, 1), slice(1, 2)) if last_bank else (slice(0, 2),):
+                    nc.vector.tensor_tensor(
+                        score[g][:, ts, m_cols], y3[u, g][:, ts, :], score[g][:, ts, m_cols], ALU.max
+                    )
+                    nc.sync.dma_start(out_rows[g][:, ts, m_cols], score[g][:, ts, m_cols])

from contextlib import ExitStack

import concourse.mybir as mybir

K, T, S, H, M, N = 1536, 4096, 1024, 512, 512, 768
FLOPS = 2 * K * H * S * 2 + 2 * H * N * M

F32 = mybir.dt.float32
BF16 = mybir.dt.bfloat16
I32 = mybir.dt.int32
U32 = mybir.dt.uint32
U16 = mybir.dt.uint16
U8 = mybir.dt.uint8
FP8X4 = mybir.dt.float8_e4m3fn_x4
FP4X4 = mybir.dt.float4_e2m1fn_x4
ACT = mybir.ActivationFunctionType
ALU = mybir.AluOpType

P = 128
PACK = 4
PASSES = K // (P * PACK)
LAST = PASSES - 1
BLOCKS = 16
QUADRANTS = 4
GROUP = 16
BANK = 512
S_HALVES = S // BANK
M_HALF = M // 2
N_HALF = N // 2
N_PAIRS = N // (2 * P)
LINE = 4

PARKED = (4, 68, 112)
TAB_CUT = (T // 2, 3 * T // 4, 3 * T // 8)
WHOLE_LOOKS = 2
EARLY_SETS = 2
W3_FIRST = 512


def tile_list_arm_leak_scores_kernel(
    tc, tab_words, tab_scales, offs, offs2, w1, w2_words, w2_scales, b2, sc, th, gain, w3, low, out
):
    nc = tc.nc
    with ExitStack() as ctx:
        sb = ctx.enter_context(tc.tile_pool(name="sb", bufs=1))
        psum = ctx.enter_context(tc.psum_pool(name="psum", bufs=1))

        def sbt(name, shape, dtype):
            return sb.tile(shape, dtype, name=name, align_bytes=64)

        tab_sc = sbt("tab_sc", [P, T], U8)
        nc.vector.memset(tab_sc[:].bitcast(I32), 0)
        w2_sc_raw = sbt("w2_sc_raw", [P, PASSES, H], U8)
        nc.vector.memset(w2_sc_raw[:].bitcast(I32), 0)
        v_sc = []
        for a in range(PASSES):
            v_sc.append(sbt(f"v_sc{a}", [P, S], U8))
            nc.vector.memset(v_sc[a][:].bitcast(I32), 0)

        idx = sbt("idx", [P, S // GROUP], U16)
        nc.sync.dma_start(idx[:], offs)
        tab = [sbt(f"tab{a}", [P, T], U32) for a in range(PASSES)]

        def load_tab(a, first, end):
            words = tab_words[a].rearrange("p t i -> p (t i)").bitcast(I32)
            nc.sync.dma_start(tab[a][:, first:end].bitcast(I32), words[:, first:end])

        load_tab(0, 0, TAB_CUT[0])
        for a in range(PASSES):
            nc.sync.dma_start(tab_sc[PARKED[a] : PARKED[a] + BLOCKS, :].bitcast(I32), tab_scales[a].bitcast(I32))
        w2_raw = sbt("w2_raw", [P, PASSES, H], U16)
        nc.sync.dma_start(w2_raw[:].bitcast(I32), w2_words.rearrange("a p c -> p a c").bitcast(I32))
        load_tab(0, TAB_CUT[0], T)
        for q in range(QUADRANTS):
            nc.sync.dma_start(
                w2_sc_raw[32 * q : 32 * q + 4, :, :].bitcast(I32),
                w2_scales[:, 4 * q : 4 * q + 4, :].rearrange("a r c -> r a c").bitcast(I32),
            )
        load_tab(1, 0, TAB_CUT[1])

        picked_sc = sbt("picked_sc", [P, S], U8)
        nc.vector.tensor_copy(picked_sc[:], tab_sc[:].indirect(idx[:]))
        w2_codes = sbt("w2_codes", [P, PASSES, H], U16)
        nc.vector.tensor_copy(
            w2_codes[:].rearrange("p a (i m) -> p a i m", i=PACK),
            w2_raw[:].rearrange("p a (m i) -> p a i m", i=PACK),
        )
        w2_sc = sbt("w2_sc", [P, PASSES, H], U8)
        for a in range(PASSES):
            nc.vector.tensor_copy(
                w2_sc[:, a, :].rearrange("p (i m) -> p i m", i=PACK),
                w2_sc_raw[:, a, :].rearrange("p (m i) -> p i m", i=PACK),
            )

        def place_scales(a):
            for q in range(QUADRANTS):
                rows = slice(PARKED[a] + 4 * q, PARKED[a] + 4 * q + 4)
                nc.sync.dma_start(v_sc[a][32 * q : 32 * q + 4, :].bitcast(I32), picked_sc[rows, :].bitcast(I32))

        def load_rows(name, vec):
            by_set = sbt(name, [P, PACK], F32)
            nc.sync.dma_start(by_set[:], vec.rearrange("(p i) -> p i", i=PACK))
            return by_set

        place_scales(0)
        load_tab(1, TAB_CUT[1], T)
        load_tab(2, 0, TAB_CUT[2])
        place_scales(1)
        b2_sb = load_rows("b2_sb", b2)
        load_tab(2, TAB_CUT[2], T)
        place_scales(2)

        w1_rows = w1.rearrange("(a p j) c -> a p j c", p=P, j=PACK)
        w1_raw = []
        for a in range(LAST):
            w1_raw.append(sbt(f"w1_raw{a}", [P, PACK, H], F32))
            nc.sync.dma_start(w1_raw[a][:], w1_rows[a])
        w1_last = []
        for half in range(2):
            w1_last.append(sbt(f"w1_last{half}", [P, PACK, H // 2], F32))
            nc.sync.dma_start(w1_last[half][:], w1_rows[LAST][:, :, half * (H // 2) : (half + 1) * (H // 2)])
        idx2 = sbt("idx2", [P, M // GROUP], U16)
        nc.sync.dma_start(idx2[:], offs2)
        sc_sb = load_rows("sc_sb", sc)
        th_sb = load_rows("th_sb", th)
        gain_sb = load_rows("gain_sb", gain)
        w3_rows = w3.rearrange("(p j) n -> p j n", j=PACK)
        w3_raw = []
        for half in range(2):
            w3_raw.append(sbt(f"w3_raw{half}", [P, PACK, N_HALF], F32))
            nc.sync.dma_start(w3_raw[half][:], w3_rows[:, :, half * N_HALF : (half + 1) * N_HALF])
        low_rows = low.rearrange("(g t p) m -> g p t m", t=2, p=P)
        out_rows = out.rearrange("(g t p) m -> g p t m", t=2, p=P)
        score = []
        for g in range(N_PAIRS):
            score.append(sbt(f"score{g}", [P, 2, M], F32))
            nc.sync.dma_start(score[g][:], low_rows[g])

        y2 = {}
        v_codes = {}
        for a in range(PASSES):
            for s in range(S_HALVES):
                v_codes[a, s] = sbt(f"v_codes{a}_{s}", [P, BANK], U32)
                nc.vector.tensor_copy(
                    v_codes[a, s][:], tab[a][:].indirect(idx[:, s * (BANK // GROUP) : (s + 1) * (BANK // GROUP)])
                )
                for i in range(PACK):
                    if a == 0:
                        y2[i, s] = psum.tile([P, BANK], F32, name=f"bank{S_HALVES * i + s}")
                    nc.tensor.matmul_mx(
                        out=y2[i, s][:],
                        lhsT=w2_codes[:, a, P * i : P * (i + 1)].bitcast(FP4X4),
                        lhsT_scale=w2_sc[:, a, P * i : P * (i + 1)],
                        rhs=v_codes[a, s][:].bitcast(FP8X4),
                        rhs_scale=v_sc[a][:, s * BANK : (s + 1) * BANK],
                        start=(a == 0),
                        stop=(a == LAST),
                    )

        h = [sbt(f"h{i}", [P, S], F32) for i in range(PACK)]
        bent = sbt("bent", [P, PACK, S], F32)
        for s in range(S_HALVES):
            for i in range(PACK):
                nc.scalar.activation(
                    out=bent[:, i, s * BANK : (s + 1) * BANK], in_=y2[i, s][:], func=ACT.Tanh, bias=b2_sb[:, i : i + 1]
                )

        w1_bf = [sbt(f"w1_bf{a}", [P, PACK, P, PACK], BF16) for a in range(LAST)]
        w1_codes = [sbt(f"w1_codes{a}", [P, H], U32) for a in range(PASSES)]
        w1_sc = [sbt(f"w1_sc{a}", [P, H], U8) for a in range(PASSES)]
        for a in range(LAST):
            nc.vector.tensor_copy(
                w1_bf[a][:].rearrange("p (x y) m j -> p x m j y", y=2),
                w1_raw[a][:].rearrange("p j (m x y) -> p x m j y", x=2, y=2),
            )
            nc.vector.quantize_mx(
                out=w1_codes[a][:].bitcast(FP8X4), scales=w1_sc[a][:], in_=w1_bf[a][:].rearrange("p i m j -> p (i m j)")
            )
        w1_pair = [sbt(f"w1_pair{x}", [P, 2, P, PACK], BF16) for x in range(2)]

        def cast_last(x, half):
            nc.vector.tensor_copy(
                w1_pair[x][:, :, half * (P // 2) : (half + 1) * (P // 2), :].rearrange("p y m j -> p m j y"),
                w1_last[half][:].rearrange("p j (m i) -> p m j i", i=PACK)[:, :, :, 2 * x : 2 * x + 2],
            )

        for x in range(2):
            cast_last(x, 0)

        y1 = {}

        def y1_pass(i, s, a, stop):
            nc.tensor.matmul_mx(
                out=y1[i, s][:],
                lhsT=w1_codes[a][:, P * i : P * (i + 1)].bitcast(FP8X4),
                lhsT_scale=w1_sc[a][:, P * i : P * (i + 1)],
                rhs=v_codes[a, s][:].bitcast(FP8X4),
                rhs_scale=v_sc[a][:, s * BANK : (s + 1) * BANK],
                start=(a == 0),
                stop=stop,
            )

        for s in range(S_HALVES):
            for i in range(PACK):
                y1[i, s] = psum.tile([P, BANK], F32, name=f"bank{S_HALVES * i + s}")
                y1_pass(i, s, 0, False)
        for x in range(2):
            cast_last(x, 1)
            nc.vector.quantize_mx(
                out=w1_codes[LAST][:, 2 * P * x : 2 * P * (x + 1)].bitcast(FP8X4),
                scales=w1_sc[LAST][:, 2 * P * x : 2 * P * (x + 1)],
                in_=w1_pair[x][:].rearrange("p y m j -> p (y m j)"),
            )
        for i in range(PACK):
            order = (LAST - 1, LAST) if i < EARLY_SETS else (LAST, LAST - 1)
            for s in range(S_HALVES):
                for a in order:
                    y1_pass(i, s, a, a == order[-1])
            for s in range(S_HALVES):
                s_cols = slice(s * BANK, (s + 1) * BANK)
                nc.vector.tensor_tensor(h[i][:, s_cols], y1[i, s][:], bent[:, i, s_cols], ALU.add)

        w3_bf = sbt("w3_bf", [P, N, PACK], BF16)
        for half in range(2):
            nc.gpsimd.tensor_scalar(
                w3_bf[:, half * N_HALF : (half + 1) * N_HALF, :],
                w3_raw[half][:].rearrange("p j n -> p n j"),
                1.0,
                0.0,
                ALU.mult,
                ALU.add,
            )
        w3_codes = sbt("w3_codes", [P, N], U32)
        w3_sc = sbt("w3_sc", [P, N], U8)
        for ns in (slice(0, W3_FIRST), slice(W3_FIRST, N)):
            nc.vector.quantize_mx(
                out=w3_codes[:, ns].bitcast(FP8X4),
                scales=w3_sc[:, ns],
                in_=w3_bf[:, ns, :].rearrange("p n j -> p (n j)"),
            )

        e_rows = sbt("e_rows", [P, PACK, M], BF16)

        def look(i, m_cols, gate, hp, buffer, gain_on_scalar):
            picks = idx2[:, m_cols.start // GROUP : m_cols.stop // GROUP]
            nc.scalar.activation(
                out=gate,
                in_=h[i][:].indirect(picks),
                func=ACT.Sigmoid,
                bias=th_sb[:, i : i + 1],
                scale=sc_sb[:, i : i + 1],
            )
            nc.scalar.activation(out=hp, in_=h[i][:].indirect(picks), func=ACT.Copy)
            bounded = sbt(buffer, [P, m_cols.stop - m_cols.start], F32)
            nc.vector.tensor_tensor(bounded[:], gate, hp, ALU.min)
            if gain_on_scalar:
                nc.scalar.activation(
                    out=e_rows[:, i, m_cols], in_=bounded[:], func=ACT.Copy, scale=gain_sb[:, i : i + 1]
                )
            else:
                nc.vector.tensor_scalar(e_rows[:, i, m_cols], bounded[:], gain_sb[:, i : i + 1], None, ALU.mult)

        whole = sbt("whole", [P, WHOLE_LOOKS, 2, M], F32)
        for i in range(WHOLE_LOOKS):
            look(i, slice(0, M), whole[:, i, 0, :], whole[:, i, 1, :], f"bounded{i}", False)

        looked_buffer = ("halved", "bent")
        bounded_buffer = (("bounded2", "bounded3"), ("bounded3", "e_bf0"))
        y3 = {}
        for u in range(2):
            m_cols = slice(u * M_HALF, (u + 1) * M_HALF)
            looked = sbt(looked_buffer[u], [P, PACK - WHOLE_LOOKS, 2, M_HALF], F32)
            for late, i in enumerate(range(WHOLE_LOOKS, PACK)):
                very_last = u == 1 and i == PACK - 1
                look(i, m_cols, looked[:, late, 0, :], looked[:, late, 1, :], bounded_buffer[u][late], very_last)
            e_bf = sbt(f"e_bf{u}", [P, M_HALF, PACK], BF16)
            interleave = nc.vector.tensor_copy if u == 0 else nc.scalar.copy
            interleave(
                e_bf[:].rearrange("p (c k) i -> p c i k", k=LINE),
                e_rows[:, :, m_cols].rearrange("p i (c k) -> p c i k", k=LINE),
            )
            e_codes = sbt(f"e_codes{u}", [P, M_HALF], U32)
            e_sc = sbt(f"e_sc{u}", [P, M_HALF], U8)
            nc.vector.quantize_mx(
                out=e_codes[:].bitcast(FP8X4), scales=e_sc[:], in_=e_bf[:].rearrange("p m i -> p (m i)")
            )
            for g in range(N_PAIRS):
                y3[u, g] = psum.tile([P, 2, M_HALF], F32, name=f"bank{N_PAIRS * u + g}")
                for t in range(2):
                    ns = slice(P * (2 * g + t), P * (2 * g + t + 1))
                    nc.tensor.matmul_mx(
                        out=y3[u, g][:, t, :],
                        lhsT=w3_codes[:, ns].bitcast(FP8X4),
                        lhsT_scale=w3_sc[:, ns],
                        rhs=e_codes[:].bitcast(FP8X4),
                        rhs_scale=e_sc[:],
                        start=True,
                        stop=True,
                    )

        for u in range(2):
            m_cols = slice(u * M_HALF, (u + 1) * M_HALF)
            for g in range(N_PAIRS):
                last_bank = u == 1 and g == N_PAIRS - 1
                for ts in (slice(0, 1), slice(1, 2)) if last_bank else (slice(0, 2),):
                    nc.vector.tensor_tensor(
                        score[g][:, ts, m_cols], y3[u, g][:, ts, :], score[g][:, ts, m_cols], ALU.max
                    )
                    nc.sync.dma_start(out_rows[g][:, ts, m_cols], score[g][:, ts, m_cols])
